import numpy as np
import ml_dtypes


def mxq(x, axis, fmt="e4m3"):
    dtype, down = {"e4m3": (ml_dtypes.float8_e4m3fn, 7), "e5m2": (ml_dtypes.float8_e5m2, 14)}[fmt]
    v = np.moveaxis(np.asarray(x, np.float32).astype(ml_dtypes.bfloat16).astype(np.float64), axis, -1)
    blocks = v.reshape(v.shape[:-1] + (-1, 32))
    amax = np.abs(blocks).max(-1, keepdims=True)
    byte = np.maximum(np.where(amax > 0, np.frexp(amax)[1] - 1 + 127, 0) - down, 1)
    scale = np.exp2(byte - 127.0)
    codes = (blocks / scale).astype(np.float32).astype(dtype).astype(np.float64)
    return np.moveaxis((codes * scale).reshape(v.shape), -1, axis)


WIDE = False


def mx_kscale(k):
    if not WIDE:
        return np.ones(k)
    levels = np.array([10, -10, 5, -5, 0])
    if k % 512:
        return np.exp2(np.random.permutation(np.resize(levels, k // 32))).repeat(32)
    a = np.empty((k // 512, 16))
    for p in range(k // 512):
        a[p, :8] = np.random.permutation(np.resize(levels, 8))
        for g in range(8):
            far = levels[np.abs(levels - a[p, g]) >= 10]
            a[p, g + 8] = far[np.random.randint(len(far))]
    return np.exp2(a.ravel()).repeat(32)


def f64(x):
    return np.asarray(x).astype(np.float64)


def striped(idx):
    return np.tile(idx.reshape(-1, 16).T, (8, 1)).astype(np.uint16)


def unstriped(offs):
    return offs[:16].T.reshape(-1).astype(np.int64)


def striped8(idx):
    return np.concatenate([x.reshape(-1, 16).T for x in idx]).astype(np.uint16)


def runs(offs, k):
    lists = np.stack([offs[16 * r : 16 * r + 16].T.reshape(-1) for r in range(8)]).astype(np.int64)
    return lists[np.arange(k) % 512 // 64]


def pack_weight(w):
    k, n = w.shape
    w = f64(np.asarray(w, np.float32).astype(ml_dtypes.bfloat16)).reshape(k // 32, 32, n)
    amax = np.abs(w).max(1)
    byte = np.clip(np.where(amax > 0, np.frexp(amax)[1] - 1 + 127 - 7, 1), 1, 254)
    scaled = (w * np.exp2(127.0 - byte)[:, None, :]).reshape(k, n).astype(np.float32)
    words = np.ascontiguousarray(scaled.reshape(k // 512, 128, 4, n).transpose(0, 1, 3, 2)).astype(ml_dtypes.float8_e4m3fn).view(np.uint8)
    return words, np.ascontiguousarray(byte.astype(np.uint8).reshape(k // 512, 16, n))


def unpack_weight(words, scales):
    g, p, n, _ = words.shape
    vals = np.ascontiguousarray(words).view(ml_dtypes.float8_e4m3fn).astype(np.float64) * np.repeat(np.exp2(scales.astype(np.float64) - 127.0), 8, axis=1)[..., None]
    return vals.transpose(0, 1, 3, 2).reshape(g * 512, n)


def sigmoid(v):
    return 1.0 / (1.0 + np.exp(-np.maximum(v, -700.0)))


K, T, S, H, J, C = 512, 2048, 256, 512, 512, 512


def setup_inputs():
    n = np.random.standard_normal
    s = mx_kscale(K)[:, None]
    packed_xT = pack_weight(n((K, T)) * s)
    return {
        "x_words": packed_xT[0],
        "x_scales": packed_xT[1],
        "w1": (n((K, H)) / np.sqrt(K) / s).astype(np.float32),
        "tab": n((H, J)).astype(np.float32),
        "gs": (np.random.uniform(0.5, 1.5, (K, 1)) / s).astype(np.float32),
        "offs": striped(np.random.permutation(T)[:S]),
        "n1": striped(np.random.randint(0, J, S)),
        "n2": striped(np.random.permutation(S)),
        "ca": striped(np.random.permutation(T)[:C]),
        "hc": striped8(np.random.randint(0, T, (8, C))),
        "n3": striped8(np.stack([np.random.permutation(S) for _ in range(8)])),
        "n4": striped8(np.stack([np.random.permutation(S) for _ in range(8)])),
    }


def reference(x_words, x_scales, w1, tab, gs, offs, n1, n2, ca, hc, n3, n4):
    x_ca = unpack_weight(x_words, x_scales)[:, unstriped(ca)]
    xq = unpack_weight(x_words, x_scales)[:, unstriped(offs)]
    y = mxq(f64(w1), 0, "e4m3").T @ xq
    z = f64(gs) * (np.maximum(y + f64(tab)[:, unstriped(n1)], y[:, unstriped(n2)]))
    zq = mxq(z, 0, "e4m3")
    a = 0.0625 * (x_ca.T @ zq)
    x_hc = unpack_weight(x_words, x_scales)[np.arange(K)[:, None], runs(hc, K)]
    b = 0.0625 * (x_hc.T @ zq)
    return a * (sigmoid(b[np.arange(C)[:, None], runs(n4, C)])) - (0.5 * (a[np.arange(C)[:, None], runs(n3, C)]))

@@ -1,0 +1,204 @@
+from contextlib import ExitStack
+
+import concourse.mybir as mybir
+
+K, T, S, H, J, C = 512, 2048, 256, 512, 512, 512
+FLOPS = 2 * K * H * S + 2 * 2 * K * C * S
+
+F32 = mybir.dt.float32
+BF16 = mybir.dt.bfloat16
+I32 = mybir.dt.int32
+U32 = mybir.dt.uint32
+U16 = mybir.dt.uint16
+U8 = mybir.dt.uint8
+FP8X4 = mybir.dt.float8_e4m3fn_x4
+ACT = mybir.ActivationFunctionType
+ALU = mybir.AluOpType
+
+P = 128
+PACK = 4
+HALF = S // 2
+LIST_HALF = HALF // 16
+RUN = 8
+
+
+def tile_picked_cdhgatebkind_none_p_kernel(
+    tc, x_words, x_scales, w1, tab, gs, offs, n1, n2, ca, hc, n3, n4, out
+):
+    nc = tc.nc
+    with ExitStack() as ctx:
+        keep = ctx.enter_context(tc.tile_pool(name="keep", bufs=1))
+        psum = ctx.enter_context(tc.psum_pool(name="psum", bufs=1))
+
+        def load_list(name, src):
+            tile = keep.tile(list(src.shape), U16, name=name)
+            nc.sync.dma_start(tile[:], src)
+            return tile
+
+        def dealt(view):
+            return view.rearrange("p (t g q) -> p g t q", t=PACK, g=16)
+
+        def in_order(view):
+            return view.rearrange("p (g t q) -> p g t q", t=PACK, g=16)
+
+        scale_win = keep.tile([P, T], U8, name="scale_win")
+        nc.vector.memset(scale_win[:].bitcast(I32), 0)
+        sixteenth = keep.tile([P, 1], F32, name="sixteenth")
+        nc.vector.memset(sixteenth[:], 0.0625)
+
+        w_rows = w1.rearrange("(p j) c -> p j c", j=PACK)
+
+        def load_w(h):
+            raw = keep.tile([P, PACK, H // 2], F32, name=f"w_raw{h}")
+            nc.sync.dma_start(raw[:], w_rows[:, :, h * (H // 2) : (h + 1) * (H // 2)])
+            return raw
+
+        w_raw = [load_w(0)]
+        rows = x_scales[0].bitcast(I32).rearrange("(q r) c -> r q c", r=4)
+        win_i32 = scale_win[:].bitcast(I32)
+        for r in range(2):
+            nc.sync.dma_start(win_i32[r:P:32, :], rows[r])
+        for r in range(2, 4):
+            nc.sync.dma_start(win_i32[r:P:16, :], rows[r].unsqueeze(1).to_broadcast([4, 2, T // 4]))
+        hc_l = load_list("hc_l", hc)
+        offs_l = load_list("offs_l", offs)
+        w_raw.append(load_w(1))
+        word_win = keep.tile([P, T], I32, name="word_win")
+        nc.sync.dma_start(word_win[:], x_words[0].rearrange("p n t -> p (n t)").bitcast(I32))
+        ca_l = load_list("ca_l", ca)
+        n1_l = load_list("n1_l", n1)
+        n2_l = load_list("n2_l", n2)
+
+        tab_rows = tab.rearrange("(p t) c -> t p c", t=PACK)
+        tab_win = []
+        for t in range(PACK):
+            win = keep.tile([P, J], F32, name=f"tab_win{t}")
+            nc.sync.dma_start(win[:], tab_rows[t])
+            tab_win.append(win)
+        gs_t = keep.tile([P, PACK], F32, name="gs_t")
+        nc.sync.dma_start(gs_t[:], gs.rearrange("(p t) o -> p (t o)", t=PACK))
+        n4_l = load_list("n4_l", n4)
+        n3_l = load_list("n3_l", n3)
+
+        hc_bytes = keep.tile([P, C], U8, name="hc_bytes", align_bytes=64)
+        nc.vector.tensor_copy(hc_bytes[:], scale_win[:].indirect(hc_l[:]))
+        hc_odd = keep.tile([P, C], U8, name="hc_odd", align_bytes=64)
+        hc_scales = keep.tile([P, C], U8, name="hc_scales", align_bytes=64)
+        xq_scales = keep.tile([P, S], U8, name="xq_scales", align_bytes=64)
+        nc.vector.tensor_copy(xq_scales[:], scale_win[:].indirect(offs_l[:]))
+        nc.vector.tensor_copy(dealt(hc_odd[:].bitcast(I32)), in_order(hc_bytes[:].bitcast(I32)))
+        nc.vector.tensor_copy(dealt(hc_scales[:].bitcast(I32)), in_order(hc_bytes[:].bitcast(I32)))
+        for r in range(2, 4):
+            nc.sync.dma_start(hc_scales[:].bitcast(I32)[r:P:32, :], hc_odd[:].bitcast(I32)[16 + r : P : 32, :])
+        ca_scales = keep.tile([P, C], U8, name="ca_scales", align_bytes=64)
+        nc.vector.tensor_copy(dealt(ca_scales[:]), scale_win[:].indirect(ca_l[:]))
+
+        w_bf = keep.tile([P, H * PACK], BF16, name="w_bf", align_bytes=64)
+        w_view = w_bf[:].rearrange("p (t m j) -> p m t j", t=PACK, j=PACK)
+        for h in range(2):
+            nc.scalar.activation(
+                w_view[:, 64 * h : 64 * (h + 1)],
+                w_raw[h][:].rearrange("p j (m t) -> p m t j", t=PACK),
+                ACT.Copy,
+            )
+        w_words = keep.tile([P, H], U32, name="w_words", align_bytes=64)
+        w_scales = keep.tile([P, H], U8, name="w_scales", align_bytes=64)
+        nc.vector.quantize_mx(out=w_words[:].bitcast(FP8X4), scales=w_scales[:], in_=w_bf[:])
+
+        words = word_win[:].bitcast(U32)
+        xq_words = keep.tile([P, S], U32, name="xq_words", align_bytes=64)
+        nc.vector.tensor_copy(xq_words[:], words.indirect(offs_l[:]))
+
+        y_ps = []
+        for t in range(PACK):
+            bank = psum.tile([P, S], F32, name=f"y_ps{t}", tag=f"ya{t}")
+            cols = slice(t * P, (t + 1) * P)
+            nc.tensor.matmul_mx(
+                out=bank[:],
+                lhsT=w_words[:, cols].bitcast(FP8X4),
+                lhsT_scale=w_scales[:, cols],
+                rhs=xq_words[:].bitcast(FP8X4),
+                rhs_scale=xq_scales[:],
+                start=True,
+                stop=True,
+            )
+            y_ps.append(bank)
+
+        hc_picked = keep.tile([P, C], U32, name="hc_picked", align_bytes=64)
+        nc.vector.tensor_copy(hc_picked[:], words.indirect(hc_l[:]))
+        ca_words = keep.tile([P, C], U32, name="ca_words", align_bytes=64)
+        nc.vector.tensor_copy(dealt(ca_words[:]), words.indirect(ca_l[:]))
+        hc_words = keep.tile([P, C], U32, name="hc_words", align_bytes=64)
+        nc.vector.tensor_copy(dealt(hc_words[:].bitcast(I32)), in_order(hc_picked[:].bitcast(I32)))
+
+        y_win, first, second = [], [], []
+        for t in range(PACK):
+            kind = keep.tile([P, S], F32, name=f"kind{t}")
+            nc.scalar.activation(kind[:], tab_win[t][:].indirect(n1_l[:]), ACT.Copy)
+            win = keep.tile([P, S], F32, name=f"y_win{t}")
+            nc.scalar.activation(win[:], y_ps[t][:], ACT.Copy)
+            summed = keep.tile([P, S], F32, name=f"first{t}")
+            nc.vector.tensor_tensor(summed[:], win[:], kind[:], ALU.add)
+            y_win.append(win)
+            first.append(summed)
+            second.append(keep.tile([P, S], F32, name=f"second{t}"))
+
+        z_words = keep.tile([P, S], U32, name="z_words", align_bytes=64)
+        z_scales = keep.tile([P, S], U8, name="z_scales", align_bytes=64)
+        for h in range(2):
+            cols = slice(h * HALF, (h + 1) * HALF)
+            larger = keep.tile([P, PACK, HALF], F32, name=f"larger{h}")
+            for t in range(PACK):
+                nc.scalar.activation(
+                    second[t][:, cols], y_win[t][:].indirect(n2_l[:, h * LIST_HALF : (h + 1) * LIST_HALF]), ACT.Copy
+                )
+                nc.vector.tensor_tensor(larger[:, t, :], first[t][:, cols], second[t][:, cols], ALU.max)
+            z_bf = keep.tile([P, HALF * PACK], BF16, name=f"z_bf{h}", align_bytes=64)
+            nc.vector.tensor_tensor(
+                z_bf[:].rearrange("p (c i t) -> p c t i", i=4, t=PACK),
+                larger[:].rearrange("p t (c i) -> p c t i", i=4),
+                gs_t[:].unsqueeze(1).unsqueeze(3).to_broadcast([P, HALF // 4, PACK, 4]),
+                ALU.mult,
+            )
+            nc.vector.quantize_mx(out=z_words[:, cols].bitcast(FP8X4), scales=z_scales[:, cols], in_=z_bf[:])
+
+        a_ps = [psum.tile([P, S], F32, name=f"a_ps{t}", tag=f"ya{t}") for t in range(PACK)]
+        b_ps = [psum.tile([P, S], F32, name=f"b_ps{t}", tag=f"b{t}") for t in range(PACK)]
+        for h in range(2):
+            cols = slice(h * HALF, (h + 1) * HALF)
+            for t in range(PACK):
+                rows_t = slice(t * P, (t + 1) * P)
+                for bank, cand_words, cand_scales in ((b_ps[t], hc_words, hc_scales), (a_ps[t], ca_words, ca_scales)):
+                    nc.tensor.matmul_mx(
+                        out=bank[:, cols],
+                        lhsT=cand_words[:, rows_t].bitcast(FP8X4),
+                        lhsT_scale=cand_scales[:, rows_t],
+                        rhs=z_words[:, cols].bitcast(FP8X4),
+                        rhs_scale=z_scales[:, cols],
+                        start=True,
+                        stop=True,
+                    )
+
+        out_rows = out.rearrange("(g t q) j -> t g q j", t=PACK, q=RUN)
+        for t in range(PACK):
+            b_win = keep.tile([P, S], F32, name=f"b_win{t}")
+            nc.vector.tensor_copy(b_win[:], b_ps[t][:])
+            a_win = keep.tile([P, S], F32, name=f"a_win{t}")
+            nc.vector.tensor_scalar(a_win[:], a_ps[t][:], 0.0625, None, ALU.mult)
+            gate = keep.tile([P, S], F32, name=f"gate{t}")
+            other = keep.tile([P, S], F32, name=f"other{t}")
+            for h in range(2):
+                cols = slice(h * HALF, (h + 1) * HALF)
+                part = slice(h * LIST_HALF, (h + 1) * LIST_HALF)
+                nc.scalar.activation(
+                    gate[:, cols], b_win[:].indirect(n4_l[:, part]), ACT.Sigmoid, scale=sixteenth[:]
+                )
+            for h in range(2):
+                cols = slice(h * HALF, (h + 1) * HALF)
+                part = slice(h * LIST_HALF, (h + 1) * LIST_HALF)
+                nc.scalar.activation(other[:, cols], a_win[:].indirect(n3_l[:, part]), ACT.Copy)
+            gated = keep.tile([P, S], F32, name=f"gated{t}")
+            nc.vector.tensor_tensor(gated[:], a_win[:], gate[:], ALU.mult)
+            result = keep.tile([P, S], F32, name=f"result{t}")
+            nc.vector.scalar_tensor_tensor(result[:], other[:], -0.5, gated[:], ALU.mult, ALU.add)
+            nc.sync.dma_start(out_rows[t], result[:])

@@ -20,6 +20,7 @@ PACK = 4
 HALF = S // 2
 LIST_HALF = HALF // 16
 RUN = 8
+N2_ON_VECTOR = 1
 
 
 def tile_picked_cdhgatebkind_none_p_kernel(
@@ -43,8 +44,6 @@ def tile_picked_cdhgatebkind_none_p_kernel(
 
         scale_win = keep.tile([P, T], U8, name="scale_win")
         nc.vector.memset(scale_win[:].bitcast(I32), 0)
-        sixteenth = keep.tile([P, 1], F32, name="sixteenth")
-        nc.vector.memset(sixteenth[:], 0.0625)
 
         w_rows = w1.rearrange("(p j) c -> p j c", j=PACK)
 
@@ -126,79 +125,86 @@ def tile_picked_cdhgatebkind_none_p_kernel(
 
         hc_picked = keep.tile([P, C], U32, name="hc_picked", align_bytes=64)
         nc.vector.tensor_copy(hc_picked[:], words.indirect(hc_l[:]))
-        ca_words = keep.tile([P, C], U32, name="ca_words", align_bytes=64)
-        nc.vector.tensor_copy(dealt(ca_words[:]), words.indirect(ca_l[:]))
-        hc_words = keep.tile([P, C], U32, name="hc_words", align_bytes=64)
+        hc_words = keep.tile([P, C], U32, name="hc_words", tag="cand_words", align_bytes=64)
         nc.vector.tensor_copy(dealt(hc_words[:].bitcast(I32)), in_order(hc_picked[:].bitcast(I32)))
 
-        y_win, first, second = [], [], []
+        lo, hi = slice(0, S), slice(S, 2 * S)
+        yk = tab_win
+        kind = [keep.tile([P, S], F32, name=f"kind{t}") for t in range(PACK)]
+        first = [keep.tile([P, S], F32, name=f"first{t}") for t in range(PACK)]
+        second = [keep.tile([P, S], F32, name=f"second{t}") for t in range(PACK)]
         for t in range(PACK):
-            kind = keep.tile([P, S], F32, name=f"kind{t}")
-            nc.scalar.activation(kind[:], tab_win[t][:].indirect(n1_l[:]), ACT.Copy)
-            win = keep.tile([P, S], F32, name=f"y_win{t}")
-            nc.scalar.activation(win[:], y_ps[t][:], ACT.Copy)
-            summed = keep.tile([P, S], F32, name=f"first{t}")
-            nc.vector.tensor_tensor(summed[:], win[:], kind[:], ALU.add)
-            y_win.append(win)
-            first.append(summed)
-            second.append(keep.tile([P, S], F32, name=f"second{t}"))
+            nc.scalar.activation(kind[t][:], tab_win[t][:].indirect(n1_l[:]), ACT.Copy)
+            nc.scalar.activation(yk[t][:, lo], y_ps[t][:], ACT.Copy)
+        larger = keep.tile([P, PACK, S], F32, name="larger")
+        for t in range(PACK):
+            if t < N2_ON_VECTOR:
+                nc.vector.tensor_copy(second[t][:], yk[t][:].indirect(n2_l[:]))
+            nc.vector.tensor_tensor(first[t][:], yk[t][:, lo], kind[t][:], ALU.add)
+            if t < N2_ON_VECTOR:
+                nc.vector.tensor_tensor(larger[:, t, :], first[t][:], second[t][:], ALU.max)
 
         z_words = keep.tile([P, S], U32, name="z_words", align_bytes=64)
         z_scales = keep.tile([P, S], U8, name="z_scales", align_bytes=64)
+        b_ps = [psum.tile([P, S], F32, name=f"b_ps{t}", tag=f"b{t}") for t in range(PACK)]
         for h in range(2):
             cols = slice(h * HALF, (h + 1) * HALF)
-            larger = keep.tile([P, PACK, HALF], F32, name=f"larger{h}")
-            for t in range(PACK):
+            for t in range(N2_ON_VECTOR, PACK):
                 nc.scalar.activation(
-                    second[t][:, cols], y_win[t][:].indirect(n2_l[:, h * LIST_HALF : (h + 1) * LIST_HALF]), ACT.Copy
+                    second[t][:, cols], yk[t][:].indirect(n2_l[:, h * LIST_HALF : (h + 1) * LIST_HALF]), ACT.Copy
                 )
-                nc.vector.tensor_tensor(larger[:, t, :], first[t][:, cols], second[t][:, cols], ALU.max)
+                nc.vector.tensor_tensor(larger[:, t, cols], first[t][:, cols], second[t][:, cols], ALU.max)
             z_bf = keep.tile([P, HALF * PACK], BF16, name=f"z_bf{h}", align_bytes=64)
             nc.vector.tensor_tensor(
                 z_bf[:].rearrange("p (c i t) -> p c t i", i=4, t=PACK),
-                larger[:].rearrange("p t (c i) -> p c t i", i=4),
+                larger[:, :, cols].rearrange("p t (c i) -> p c t i", i=4),
                 gs_t[:].unsqueeze(1).unsqueeze(3).to_broadcast([P, HALF // 4, PACK, 4]),
                 ALU.mult,
             )
             nc.vector.quantize_mx(out=z_words[:, cols].bitcast(FP8X4), scales=z_scales[:, cols], in_=z_bf[:])
-
-        a_ps = [psum.tile([P, S], F32, name=f"a_ps{t}", tag=f"ya{t}") for t in range(PACK)]
-        b_ps = [psum.tile([P, S], F32, name=f"b_ps{t}", tag=f"b{t}") for t in range(PACK)]
-        for h in range(2):
-            cols = slice(h * HALF, (h + 1) * HALF)
             for t in range(PACK):
                 rows_t = slice(t * P, (t + 1) * P)
-                for bank, cand_words, cand_scales in ((b_ps[t], hc_words, hc_scales), (a_ps[t], ca_words, ca_scales)):
-                    nc.tensor.matmul_mx(
-                        out=bank[:, cols],
-                        lhsT=cand_words[:, rows_t].bitcast(FP8X4),
-                        lhsT_scale=cand_scales[:, rows_t],
-                        rhs=z_words[:, cols].bitcast(FP8X4),
-                        rhs_scale=z_scales[:, cols],
-                        start=True,
-                        stop=True,
-                    )
+                nc.tensor.matmul_mx(
+                    out=b_ps[t][:, cols],
+                    lhsT=hc_words[:, rows_t].bitcast(FP8X4),
+                    lhsT_scale=hc_scales[:, rows_t],
+                    rhs=z_words[:, cols].bitcast(FP8X4),
+                    rhs_scale=z_scales[:, cols],
+                    start=True,
+                    stop=True,
+                )
+
+        ag = [keep.tile([P, 2 * S], F32, name=f"ag{t}") for t in range(PACK)]
+        ca_words = keep.tile([P, C], U32, name="ca_words", tag="cand_words", align_bytes=64)
+        for t in range(PACK):
+            nc.vector.tensor_scalar(yk[t][:, lo], b_ps[t][:], 0.0625, None, ALU.mult)
+            nc.scalar.activation(ag[t][:, hi], yk[t][:].indirect(n4_l[:]), ACT.Sigmoid)
+            if t == 1:
+                nc.vector.tensor_copy(dealt(ca_words[:]), words.indirect(ca_l[:]))
 
         out_rows = out.rearrange("(g t q) j -> t g q j", t=PACK, q=RUN)
         for t in range(PACK):
-            b_win = keep.tile([P, S], F32, name=f"b_win{t}")
-            nc.vector.tensor_copy(b_win[:], b_ps[t][:])
-            a_win = keep.tile([P, S], F32, name=f"a_win{t}")
-            nc.vector.tensor_scalar(a_win[:], a_ps[t][:], 0.0625, None, ALU.mult)
-            gate = keep.tile([P, S], F32, name=f"gate{t}")
-            other = keep.tile([P, S], F32, name=f"other{t}")
-            for h in range(2):
-                cols = slice(h * HALF, (h + 1) * HALF)
-                part = slice(h * LIST_HALF, (h + 1) * LIST_HALF)
-                nc.scalar.activation(
-                    gate[:, cols], b_win[:].indirect(n4_l[:, part]), ACT.Sigmoid, scale=sixteenth[:]
-                )
-            for h in range(2):
-                cols = slice(h * HALF, (h + 1) * HALF)
-                part = slice(h * LIST_HALF, (h + 1) * LIST_HALF)
-                nc.scalar.activation(other[:, cols], a_win[:].indirect(n3_l[:, part]), ACT.Copy)
+            rows_t = slice(t * P, (t + 1) * P)
+            a_ps = psum.tile([P, S], F32, name=f"a_ps{t}", tag=f"ya{t}")
+            nc.tensor.matmul_mx(
+                out=a_ps[:],
+                lhsT=ca_words[:, rows_t].bitcast(FP8X4),
+                lhsT_scale=ca_scales[:, rows_t],
+                rhs=z_words[:].bitcast(FP8X4),
+                rhs_scale=z_scales[:],
+                start=True,
+                stop=True,
+            )
+            nc.vector.tensor_scalar(ag[t][:, lo], a_ps[:], 0.0625, None, ALU.mult)
             gated = keep.tile([P, S], F32, name=f"gated{t}")
-            nc.vector.tensor_tensor(gated[:], a_win[:], gate[:], ALU.mult)
-            result = keep.tile([P, S], F32, name=f"result{t}")
-            nc.vector.scalar_tensor_tensor(result[:], other[:], -0.5, gated[:], ALU.mult, ALU.add)
-            nc.sync.dma_start(out_rows[t], result[:])
+            nc.vector.tensor_tensor(gated[:], ag[t][:, lo], ag[t][:, hi], ALU.mult)
+            other = keep.tile([P, S], F32, name=f"other{t}")
+            pieces = 2 if t == PACK - 1 else 1
+            width = S // pieces
+            for h in range(pieces):
+                cols = slice(h * width, (h + 1) * width)
+                part = slice(h * width // 16, (h + 1) * width // 16)
+                nc.scalar.activation(other[:, cols], ag[t][:].indirect(n3_l[:, part]), ACT.Copy)
+                result = keep.tile([P, width], F32, name=f"result{t}_{h}")
+                nc.vector.scalar_tensor_tensor(result[:], other[:, cols], -0.5, gated[:, cols], ALU.mult, ALU.add)
+                nc.sync.dma_start(out_rows[t][:, :, cols], result[:])

@@ -20,7 +20,7 @@ PACK = 4
 HALF = S // 2
 LIST_HALF = HALF // 16
 RUN = 8
-N2_ON_VECTOR = 1
+N2_ON_VECTOR = 2
 
 
 def tile_picked_cdhgatebkind_none_p_kernel(
@@ -140,7 +140,7 @@ def tile_picked_cdhgatebkind_none_p_kernel(
         for t in range(PACK):
             if t < N2_ON_VECTOR:
                 nc.vector.tensor_copy(second[t][:], yk[t][:].indirect(n2_l[:]))
-            nc.vector.tensor_tensor(first[t][:], yk[t][:, lo], kind[t][:], ALU.add)
+            nc.gpsimd.tensor_tensor(first[t][:], yk[t][:, lo], kind[t][:], ALU.add)
             if t < N2_ON_VECTOR:
                 nc.vector.tensor_tensor(larger[:, t, :], first[t][:], second[t][:], ALU.max)
 
@@ -197,14 +197,15 @@ def tile_picked_cdhgatebkind_none_p_kernel(
             )
             nc.vector.tensor_scalar(ag[t][:, lo], a_ps[:], 0.0625, None, ALU.mult)
             gated = keep.tile([P, S], F32, name=f"gated{t}")
-            nc.vector.tensor_tensor(gated[:], ag[t][:, lo], ag[t][:, hi], ALU.mult)
+            nc.vector.scalar_tensor_tensor(gated[:], a_ps[:], 0.0625, ag[t][:, hi], ALU.mult, ALU.mult)
             other = keep.tile([P, S], F32, name=f"other{t}")
             pieces = 2 if t == PACK - 1 else 1
             width = S // pieces
             for h in range(pieces):
                 cols = slice(h * width, (h + 1) * width)
                 part = slice(h * width // 16, (h + 1) * width // 16)
-                nc.scalar.activation(other[:, cols], ag[t][:].indirect(n3_l[:, part]), ACT.Copy)
+                nc.scalar.activation(other[:, cols], ag[t][:].indirect(n3_l[:, part]), ACT.Copy, scale=-0.5)
                 result = keep.tile([P, width], F32, name=f"result{t}_{h}")
-                nc.vector.scalar_tensor_tensor(result[:], other[:, cols], -0.5, gated[:, cols], ALU.mult, ALU.add)
+                adder = nc.vector if t >= 2 else nc.gpsimd
+                adder.tensor_tensor(result[:], other[:, cols], gated[:, cols], ALU.add)
                 nc.sync.dma_start(out_rows[t][:, :, cols], result[:])

from contextlib import ExitStack

import concourse.mybir as mybir

K, T, S, H, J, C = 512, 2048, 256, 512, 512, 512
FLOPS = 2 * K * H * S + 2 * 2 * K * C * S

F32 = mybir.dt.float32
BF16 = mybir.dt.bfloat16
I32 = mybir.dt.int32
U32 = mybir.dt.uint32
U16 = mybir.dt.uint16
U8 = mybir.dt.uint8
FP8X4 = mybir.dt.float8_e4m3fn_x4
ACT = mybir.ActivationFunctionType
ALU = mybir.AluOpType

P = 128
PACK = 4
HALF = S // 2
LIST_HALF = HALF // 16
RUN = 8
N2_ON_VECTOR = 2


def tile_picked_cdhgatebkind_none_p_kernel(
    tc, x_words, x_scales, w1, tab, gs, offs, n1, n2, ca, hc, n3, n4, out
):
    nc = tc.nc
    with ExitStack() as ctx:
        keep = ctx.enter_context(tc.tile_pool(name="keep", bufs=1))
        psum = ctx.enter_context(tc.psum_pool(name="psum", bufs=1))

        def load_list(name, src):
            tile = keep.tile(list(src.shape), U16, name=name)
            nc.sync.dma_start(tile[:], src)
            return tile

        def dealt(view):
            return view.rearrange("p (t g q) -> p g t q", t=PACK, g=16)

        def in_order(view):
            return view.rearrange("p (g t q) -> p g t q", t=PACK, g=16)

        scale_win = keep.tile([P, T], U8, name="scale_win")
        nc.vector.memset(scale_win[:].bitcast(I32), 0)

        w_rows = w1.rearrange("(p j) c -> p j c", j=PACK)

        def load_w(h):
            raw = keep.tile([P, PACK, H // 2], F32, name=f"w_raw{h}")
            nc.sync.dma_start(raw[:], w_rows[:, :, h * (H // 2) : (h + 1) * (H // 2)])
            return raw

        w_raw = [load_w(0)]
        rows = x_scales[0].bitcast(I32).rearrange("(q r) c -> r q c", r=4)
        win_i32 = scale_win[:].bitcast(I32)
        for r in range(2):
            nc.sync.dma_start(win_i32[r:P:32, :], rows[r])
        for r in range(2, 4):
            nc.sync.dma_start(win_i32[r:P:16, :], rows[r].unsqueeze(1).to_broadcast([4, 2, T // 4]))
        hc_l = load_list("hc_l", hc)
        offs_l = load_list("offs_l", offs)
        w_raw.append(load_w(1))
        word_win = keep.tile([P, T], I32, name="word_win")
        nc.sync.dma_start(word_win[:], x_words[0].rearrange("p n t -> p (n t)").bitcast(I32))
        ca_l = load_list("ca_l", ca)
        n1_l = load_list("n1_l", n1)
        n2_l = load_list("n2_l", n2)

        tab_rows = tab.rearrange("(p t) c -> t p c", t=PACK)
        tab_win = []
        for t in range(PACK):
            win = keep.tile([P, J], F32, name=f"tab_win{t}")
            nc.sync.dma_start(win[:], tab_rows[t])
            tab_win.append(win)
        gs_t = keep.tile([P, PACK], F32, name="gs_t")
        nc.sync.dma_start(gs_t[:], gs.rearrange("(p t) o -> p (t o)", t=PACK))
        n4_l = load_list("n4_l", n4)
        n3_l = load_list("n3_l", n3)

        hc_bytes = keep.tile([P, C], U8, name="hc_bytes", align_bytes=64)
        nc.vector.tensor_copy(hc_bytes[:], scale_win[:].indirect(hc_l[:]))
        hc_odd = keep.tile([P, C], U8, name="hc_odd", align_bytes=64)
        hc_scales = keep.tile([P, C], U8, name="hc_scales", align_bytes=64)
        xq_scales = keep.tile([P, S], U8, name="xq_scales", align_bytes=64)
        nc.vector.tensor_copy(xq_scales[:], scale_win[:].indirect(offs_l[:]))
        nc.vector.tensor_copy(dealt(hc_odd[:].bitcast(I32)), in_order(hc_bytes[:].bitcast(I32)))
        nc.vector.tensor_copy(dealt(hc_scales[:].bitcast(I32)), in_order(hc_bytes[:].bitcast(I32)))
        for r in range(2, 4):
            nc.sync.dma_start(hc_scales[:].bitcast(I32)[r:P:32, :], hc_odd[:].bitcast(I32)[16 + r : P : 32, :])
        ca_scales = keep.tile([P, C], U8, name="ca_scales", align_bytes=64)
        nc.vector.tensor_copy(dealt(ca_scales[:]), scale_win[:].indirect(ca_l[:]))

        w_bf = keep.tile([P, H * PACK], BF16, name="w_bf", align_bytes=64)
        w_view = w_bf[:].rearrange("p (t m j) -> p m t j", t=PACK, j=PACK)
        for h in range(2):
            nc.scalar.activation(
                w_view[:, 64 * h : 64 * (h + 1)],
                w_raw[h][:].rearrange("p j (m t) -> p m t j", t=PACK),
                ACT.Copy,
            )
        w_words = keep.tile([P, H], U32, name="w_words", align_bytes=64)
        w_scales = keep.tile([P, H], U8, name="w_scales", align_bytes=64)
        nc.vector.quantize_mx(out=w_words[:].bitcast(FP8X4), scales=w_scales[:], in_=w_bf[:])

        words = word_win[:].bitcast(U32)
        xq_words = keep.tile([P, S], U32, name="xq_words", align_bytes=64)
        nc.vector.tensor_copy(xq_words[:], words.indirect(offs_l[:]))

        y_ps = []
        for t in range(PACK):
            bank = psum.tile([P, S], F32, name=f"y_ps{t}", tag=f"ya{t}")
            cols = slice(t * P, (t + 1) * P)
            nc.tensor.matmul_mx(
                out=bank[:],
                lhsT=w_words[:, cols].bitcast(FP8X4),
                lhsT_scale=w_scales[:, cols],
                rhs=xq_words[:].bitcast(FP8X4),
                rhs_scale=xq_scales[:],
                start=True,
                stop=True,
            )
            y_ps.append(bank)

        hc_picked = keep.tile([P, C], U32, name="hc_picked", align_bytes=64)
        nc.vector.tensor_copy(hc_picked[:], words.indirect(hc_l[:]))
        hc_words = keep.tile([P, C], U32, name="hc_words", tag="cand_words", align_bytes=64)
        nc.vector.tensor_copy(dealt(hc_words[:].bitcast(I32)), in_order(hc_picked[:].bitcast(I32)))

        lo, hi = slice(0, S), slice(S, 2 * S)
        yk = tab_win
        kind = [keep.tile([P, S], F32, name=f"kind{t}") for t in range(PACK)]
        first = [keep.tile([P, S], F32, name=f"first{t}") for t in range(PACK)]
        second = [keep.tile([P, S], F32, name=f"second{t}") for t in range(PACK)]
        for t in range(PACK):
            nc.scalar.activation(kind[t][:], tab_win[t][:].indirect(n1_l[:]), ACT.Copy)
            nc.scalar.activation(yk[t][:, lo], y_ps[t][:], ACT.Copy)
        larger = keep.tile([P, PACK, S], F32, name="larger")
        for t in range(PACK):
            if t < N2_ON_VECTOR:
                nc.vector.tensor_copy(second[t][:], yk[t][:].indirect(n2_l[:]))
            nc.gpsimd.tensor_tensor(first[t][:], yk[t][:, lo], kind[t][:], ALU.add)
            if t < N2_ON_VECTOR:
                nc.vector.tensor_tensor(larger[:, t, :], first[t][:], second[t][:], ALU.max)

        z_words = keep.tile([P, S], U32, name="z_words", align_bytes=64)
        z_scales = keep.tile([P, S], U8, name="z_scales", align_bytes=64)
        b_ps = [psum.tile([P, S], F32, name=f"b_ps{t}", tag=f"b{t}") for t in range(PACK)]
        for h in range(2):
            cols = slice(h * HALF, (h + 1) * HALF)
            for t in range(N2_ON_VECTOR, PACK):
                nc.scalar.activation(
                    second[t][:, cols], yk[t][:].indirect(n2_l[:, h * LIST_HALF : (h + 1) * LIST_HALF]), ACT.Copy
                )
                nc.vector.tensor_tensor(larger[:, t, cols], first[t][:, cols], second[t][:, cols], ALU.max)
            z_bf = keep.tile([P, HALF * PACK], BF16, name=f"z_bf{h}", align_bytes=64)
            nc.vector.tensor_tensor(
                z_bf[:].rearrange("p (c i t) -> p c t i", i=4, t=PACK),
                larger[:, :, cols].rearrange("p t (c i) -> p c t i", i=4),
                gs_t[:].unsqueeze(1).unsqueeze(3).to_broadcast([P, HALF // 4, PACK, 4]),
                ALU.mult,
            )
            nc.vector.quantize_mx(out=z_words[:, cols].bitcast(FP8X4), scales=z_scales[:, cols], in_=z_bf[:])
            for t in range(PACK):
                rows_t = slice(t * P, (t + 1) * P)
                nc.tensor.matmul_mx(
                    out=b_ps[t][:, cols],
                    lhsT=hc_words[:, rows_t].bitcast(FP8X4),
                    lhsT_scale=hc_scales[:, rows_t],
                    rhs=z_words[:, cols].bitcast(FP8X4),
                    rhs_scale=z_scales[:, cols],
                    start=True,
                    stop=True,
                )

        ag = [keep.tile([P, 2 * S], F32, name=f"ag{t}") for t in range(PACK)]
        ca_words = keep.tile([P, C], U32, name="ca_words", tag="cand_words", align_bytes=64)
        for t in range(PACK):
            nc.vector.tensor_scalar(yk[t][:, lo], b_ps[t][:], 0.0625, None, ALU.mult)
            nc.scalar.activation(ag[t][:, hi], yk[t][:].indirect(n4_l[:]), ACT.Sigmoid)
            if t == 1:
                nc.vector.tensor_copy(dealt(ca_words[:]), words.indirect(ca_l[:]))

        out_rows = out.rearrange("(g t q) j -> t g q j", t=PACK, q=RUN)
        for t in range(PACK):
            rows_t = slice(t * P, (t + 1) * P)
            a_ps = psum.tile([P, S], F32, name=f"a_ps{t}", tag=f"ya{t}")
            nc.tensor.matmul_mx(
                out=a_ps[:],
                lhsT=ca_words[:, rows_t].bitcast(FP8X4),
                lhsT_scale=ca_scales[:, rows_t],
                rhs=z_words[:].bitcast(FP8X4),
                rhs_scale=z_scales[:],
                start=True,
                stop=True,
            )
            nc.vector.tensor_scalar(ag[t][:, lo], a_ps[:], 0.0625, None, ALU.mult)
            gated = keep.tile([P, S], F32, name=f"gated{t}")
            nc.vector.scalar_tensor_tensor(gated[:], a_ps[:], 0.0625, ag[t][:, hi], ALU.mult, ALU.mult)
            other = keep.tile([P, S], F32, name=f"other{t}")
            pieces = 2 if t == PACK - 1 else 1
            width = S // pieces
            for h in range(pieces):
                cols = slice(h * width, (h + 1) * width)
                part = slice(h * width // 16, (h + 1) * width // 16)
                nc.scalar.activation(other[:, cols], ag[t][:].indirect(n3_l[:, part]), ACT.Copy, scale=-0.5)
                result = keep.tile([P, width], F32, name=f"result{t}_{h}")
                adder = nc.vector if t >= 2 else nc.gpsimd
                adder.tensor_tensor(result[:], other[:, cols], gated[:, cols], ALU.add)
                nc.sync.dma_start(out_rows[t][:, :, cols], result[:])
